import numpy as np
import ml_dtypes


def mxq(x, axis, fmt="e4m3"):
    dtype, down = {"e4m3": (ml_dtypes.float8_e4m3fn, 7), "e5m2": (ml_dtypes.float8_e5m2, 14)}[fmt]
    v = np.moveaxis(np.asarray(x, np.float32).astype(ml_dtypes.bfloat16).astype(np.float64), axis, -1)
    blocks = v.reshape(v.shape[:-1] + (-1, 32))
    amax = np.abs(blocks).max(-1, keepdims=True)
    byte = np.maximum(np.where(amax > 0, np.frexp(amax)[1] - 1 + 127, 0) - down, 1)
    scale = np.exp2(byte - 127.0)
    codes = (blocks / scale).astype(np.float32).astype(dtype).astype(np.float64)
    return np.moveaxis((codes * scale).reshape(v.shape), -1, axis)


WIDE = False


def mx_kscale(k):
    if not WIDE:
        return np.ones(k)
    levels = np.array([10, -10, 5, -5, 0])
    if k % 512:
        return np.exp2(np.random.permutation(np.resize(levels, k // 32))).repeat(32)
    a = np.empty((k // 512, 16))
    for p in range(k // 512):
        a[p, :8] = np.random.permutation(np.resize(levels, 8))
        for g in range(8):
            far = levels[np.abs(levels - a[p, g]) >= 10]
            a[p, g + 8] = far[np.random.randint(len(far))]
    return np.exp2(a.ravel()).repeat(32)


def f64(x):
    return np.asarray(x).astype(np.float64)


def striped(idx):
    return np.tile(np.asarray(idx).reshape(-1, 16).T, (8, 1)).astype(np.uint16)


def unstriped(offs):
    return offs[:16].T.reshape(-1).astype(np.int64)


E2M1 = np.array([0.0, 0.5, 1.0, 1.5, 2.0, 3.0, 4.0, 6.0, -0.0, -0.5, -1.0, -1.5, -2.0, -3.0, -4.0, -6.0])


def pack_weight(w, fmt):
    k, n = w.shape
    w = f64(np.asarray(w, np.float32).astype(ml_dtypes.bfloat16)).reshape(k // 32, 32, n)
    amax = np.abs(w).max(1)
    if fmt == "e4m3":
        byte = np.frexp(amax)[1] - 1 + 127 - 7
    else:
        mant, ex = np.frexp(amax / 6.0)
        byte = np.where(mant > 0.5, ex, ex - 1) + 127
    byte = np.clip(np.where(amax > 0, byte, 1), 1, 254)
    scaled = (w * np.exp2(127.0 - byte)[:, None, :]).reshape(k, n).astype(np.float32)
    by_word = np.ascontiguousarray(scaled.reshape(k // 512, 128, 4, n).transpose(0, 1, 3, 2))
    if fmt == "e4m3":
        words = by_word.astype(ml_dtypes.float8_e4m3fn).view(np.uint8)
    else:
        c = by_word.astype(ml_dtypes.float4_e2m1fn).view(np.uint8) & 0xF
        words = (c[..., 0::2] | (c[..., 1::2] << 4)).reshape(k // 512, 128, 2 * n)
    return np.ascontiguousarray(words), np.ascontiguousarray(byte.astype(np.uint8).reshape(k // 512, 16, n))


def unpack_weight(words, scales, fmt):
    g, _, n = scales.shape
    words = np.ascontiguousarray(words).reshape(g, 128, n, -1)
    if fmt == "e4m3":
        vals = words.view(ml_dtypes.float8_e4m3fn).astype(np.float64)
    else:
        nib = np.empty((g, 128, n, 4), np.uint8)
        nib[..., 0::2] = words & 0xF
        nib[..., 1::2] = words >> 4
        vals = E2M1[nib]
    vals = vals * np.repeat(np.exp2(scales.astype(np.float64) - 127.0), 8, axis=1)[..., None]
    return vals.transpose(0, 1, 3, 2).reshape(g * 512, n)


D, T, I, Q, E = 512, 2048, 512, 128, 512


def setup_inputs():
    n = np.random.standard_normal
    idx = np.random.permutation(T)[:I]
    idx2 = np.random.permutation(T)[:I]
    idx3 = np.random.permutation(T)[:I]
    fd = mx_kscale(D)
    fi = mx_kscale(I)
    ti = np.ones(T)
    ti[idx3] = fi
    keysp = pack_weight(n((D, T)) / fd[:, None], "e4m3")
    return {
        "query": (n((D, Q)) * 0.6 / np.sqrt(D) * fd[:, None]).astype(np.float32),
        "keys_words": keysp[0],
        "keys_scales": keysp[1],
        "size": (np.random.uniform(0.5, 2.0, (1, I)) * fi).astype(np.float32),
        "vals": (n((E, T)) / ti).astype(np.float32),
        "offs": striped(idx),
        "offs2": striped(idx2),
        "offs3": striped(idx3),
    }


def reference(query, keys_words, keys_scales, size, vals, offs, offs2, offs3):
    idx = unstriped(offs)
    idx2 = unstriped(offs2)
    idx3 = unstriped(offs3)
    keysu = unpack_weight(keys_words, keys_scales, "e4m3")
    queryq = mxq(f64(query), 0, "e4m3")
    keysidxg = keysu[:, idx]
    a = queryq.T @ keysidxg
    keysidx2g = keysu[:, idx2]
    b = queryq.T @ keysidx2g
    s = np.log(np.exp(a) + np.exp(b))
    p = np.exp(s - np.max(s, axis=1, keepdims=True))
    w = p * f64(size) / np.sum(p, axis=1, keepdims=True)
    wt = w.T
    vt = f64(vals)[:, idx3].T
    wtq = mxq(wt, 0, "e4m3")
    vtq = mxq(vt, 0, "e4m3")
    o = wtq.T @ vtq
    return o

@@ -1,0 +1,158 @@
+from contextlib import ExitStack
+
+import concourse.mybir as mybir
+from concourse.masks import make_identity
+
+D, T, SLOTS, Q, E = 512, 2048, 512, 128, 512
+FLOPS = 2 * (2 * D * Q * SLOTS + SLOTS * Q * E)
+
+F32 = mybir.dt.float32
+BF16 = mybir.dt.bfloat16
+I32 = mybir.dt.int32
+U32 = mybir.dt.uint32
+U16 = mybir.dt.uint16
+U8 = mybir.dt.uint8
+FP8X4 = mybir.dt.float8_e4m3fn_x4
+ALU = mybir.AluOpType
+ACT = mybir.ActivationFunctionType
+AX = mybir.AxisListType
+
+P = 128
+PACK = 4
+BLOCKS = E // P
+
+
+def tile_attend_synonyms_kernel(tc, query, keys_words, keys_scales, size, vals, offs, offs2, offs3, out):
+    nc = tc.nc
+    with ExitStack() as ctx:
+        sb = ctx.enter_context(tc.tile_pool(name="sb", bufs=1))
+        ps = ctx.enter_context(tc.psum_pool(name="ps", bufs=1))
+        ps2 = ctx.enter_context(tc.psum_pool(name="ps2", bufs=2))
+
+        list_a = sb.tile([P, SLOTS // 16], U16, name="list_a")
+        list_b = sb.tile([P, SLOTS // 16], U16, name="list_b")
+        list_v = sb.tile([P, SLOTS // 16], U16, name="list_v")
+        kscale = sb.tile([P, T], U8, name="kscale", align_bytes=64)
+        kwords = sb.tile([P, T], U32, name="kwords", align_bytes=64)
+        qraw = sb.tile([P, PACK, Q], F32, name="qraw")
+        size_col = sb.tile([P, PACK], F32, name="size_col")
+        ident = sb.tile([P, P], F32, name="ident")
+
+        nc.vector.memset(kscale[:].bitcast(I32), 0)
+        make_identity(nc, ident[:])
+
+        nc.sync.dma_start(list_a[:], offs)
+        nc.sync.dma_start(list_b[:], offs2)
+        for quad in range(4):
+            nc.scalar.dma_start(
+                out=kscale[32 * quad : 32 * quad + 4, :].bitcast(I32),
+                in_=keys_scales[0, 4 * quad : 4 * quad + 4, :].bitcast(I32),
+            )
+        nc.sync.dma_start(out=qraw[:], in_=query.rearrange("(p j) q -> p j q", j=PACK))
+        nc.sync.dma_start(out=kwords[:].bitcast(I32), in_=keys_words[0].rearrange("p n t -> p (n t)").bitcast(I32))
+        vraw = [sb.tile([P, T], F32, name=f"vraw{b}") for b in range(BLOCKS)]
+        nc.sync.dma_start(out=vraw[0][:], in_=vals[0:P, :])
+        nc.sync.dma_start(list_v[:], offs3)
+        nc.sync.dma_start(out=size_col[:], in_=size.rearrange("o (p t) -> p (o t)", t=PACK))
+        for b in range(1, BLOCKS):
+            nc.sync.dma_start(out=vraw[b][:], in_=vals[b * P : (b + 1) * P, :])
+
+        warm = sb.tile([P, 1], F32, name="warm")
+        nc.scalar.activation(out=warm[:], in_=ident[:, 0:1], func=ACT.Exp)
+        qgrp = sb.tile([P, Q, PACK], BF16, name="qgrp", align_bytes=64)
+        nc.scalar.copy(out=qgrp[:], in_=qraw[:].rearrange("p j q -> p q j"))
+        qcodes = sb.tile([P, Q], U32, name="qcodes", align_bytes=64)
+        qscale = sb.tile([P, Q], U8, name="qscale", align_bytes=64)
+
+        gs = []
+        gw = []
+        for name, lst in (("a", list_a), ("b", list_b)):
+            g = sb.tile([P, SLOTS], U8, name=f"gs_{name}", align_bytes=64)
+            nc.vector.tensor_copy(g[:], kscale[:].indirect(lst[:]))
+            gs.append(g)
+        nc.vector.quantize_mx(out=qcodes[:].bitcast(FP8X4), scales=qscale[:], in_=qgrp[:].rearrange("p q j -> p (q j)"))
+        scores = []
+        for i, (name, lst) in enumerate((("a", list_a), ("b", list_b))):
+            g = sb.tile([P, SLOTS], U32, name=f"gw_{name}", align_bytes=64)
+            nc.vector.tensor_copy(g[:], kwords[:].indirect(lst[:]))
+            gw.append(g)
+            sc = ps.tile([P, SLOTS], F32, name=f"score_{name}")
+            nc.tensor.matmul_mx(out=sc[:], lhsT=qcodes[:].bitcast(FP8X4), lhsT_scale=qscale[:],
+                                rhs=g[:].bitcast(FP8X4), rhs_scale=gs[i][:], start=True, stop=True)
+            scores.append(sc)
+
+        size_bc = ps.tile([P, PACK, P], F32, name="size_bc")
+        for t in range(PACK):
+            nc.tensor.transpose(size_bc[:, t, :], size_col[:, t : t + 1].to_broadcast([P, P]), ident[:])
+
+        def turn(src, name):
+            words = src[:].bitcast(F32)
+            turned = ps2.tile([P, 2, P], F32, name="turned")
+            for u in range(2):
+                nc.tensor.transpose(turned[:, u, :], words[:, u : 2 * P : 2], ident[:])
+            grp = sb.tile([P, P, PACK], BF16, name=f"grp_{name}", align_bytes=64)
+            nc.scalar.copy(out=grp[:].rearrange("p c t -> p (c t)").bitcast(F32).rearrange("p (c u) -> p c u", u=2),
+                           in_=turned[:].rearrange("p u c -> p c u"))
+            return grp
+
+        def quant(grp, name):
+            codes = sb.tile([P, P], U32, name=f"codes_{name}", align_bytes=64)
+            scales = sb.tile([P, P], U8, name=f"scales_{name}", align_bytes=64)
+            nc.vector.quantize_mx(out=codes[:].bitcast(FP8X4), scales=scales[:], in_=grp[:].rearrange("p c t -> p (c t)"))
+            return codes, scales
+
+        def gather_v(b):
+            g = sb.tile([P, SLOTS], BF16, name=f"gv{b}", align_bytes=64)
+            nc.vector.tensor_copy(g[:], vraw[b][:].indirect(list_v[:]))
+            return turn(g, f"v{b}")
+
+        vg = [None] * BLOCKS
+        vq = [None] * BLOCKS
+        vg[0] = gather_v(0)
+
+        tops = sb.tile([P, 2], F32, name="tops")
+        for i in range(2):
+            nc.vector.tensor_reduce(out=tops[:, i : i + 1], in_=scores[i][:], axis=AX.X, op=ALU.max)
+        neg_top = sb.tile([P, 1], F32, name="neg_top")
+        nc.vector.tensor_reduce(out=neg_top[:], in_=tops[:], axis=AX.X, op=ALU.max, negate=True)
+        ex = []
+        for i in range(2):
+            e = sb.tile([P, SLOTS], F32, name=f"exp{i}")
+            nc.scalar.activation(out=e[:], in_=scores[i][:], func=ACT.Exp, bias=neg_top[:])
+            ex.append(e)
+        vq[0] = quant(vg[0], "v0")
+        vg[1] = gather_v(1)
+        pair = sb.tile([P, SLOTS], F32, name="pair")
+        total = sb.tile([P, 1], F32, name="total")
+        nc.vector.scalar_tensor_tensor(out=pair[:], in0=ex[0][:], scalar=1.0, in1=ex[1][:], op0=ALU.mult, op1=ALU.add,
+                                       accum_out=total[:])
+        inv = sb.tile([P, 1], F32, name="inv")
+        nc.vector.reciprocal(out=inv[:], in_=total[:])
+        vq[1] = quant(vg[1], "v1")
+        w = sb.tile([P, SLOTS], BF16, name="w", align_bytes=64)
+        nc.vector.scalar_tensor_tensor(out=w[:].rearrange("q (p t) -> q p t", t=PACK),
+                                       in0=pair[:].rearrange("q (p t) -> q p t", t=PACK), scalar=inv[:],
+                                       in1=size_bc[:].rearrange("q t p -> q p t"), op0=ALU.mult, op1=ALU.mult)
+        wg = turn(w, "w")
+        vg[2] = gather_v(2)
+        wcodes, wscales = quant(wg, "w")
+        vq[2] = quant(vg[2], "v2")
+
+        def product(acc, b):
+            nc.tensor.matmul_mx(out=acc, lhsT=wcodes[:].bitcast(FP8X4), lhsT_scale=wscales[:],
+                                rhs=vq[b][0][:].bitcast(FP8X4), rhs_scale=vq[b][1][:], start=True, stop=True)
+
+        early = ps.tile([P, 3 * P], F32, name="early")
+        for b in range(3):
+            product(early[:, b * P : (b + 1) * P], b)
+        early_sb = sb.tile([P, 3 * P], F32, name="early_sb")
+        nc.scalar.copy(out=early_sb[:], in_=early[:])
+        nc.sync.dma_start(out=out[:, 0 : 3 * P], in_=early_sb[:])
+
+        vg[3] = gather_v(3)
+        vq[3] = quant(vg[3], "v3")
+        late = ps.tile([P, P], F32, name="late")
+        product(late[:], 3)
+        late_sb = sb.tile([P, P], F32, name="late_sb")
+        nc.vector.tensor_copy(out=late_sb[:], in_=late[:])
+        nc.sync.dma_start(out=out[:, 3 * P : 4 * P], in_=late_sb[:])

@@ -27,40 +27,42 @@ def tile_attend_synonyms_kernel(tc, query, keys_words, keys_scales, size, vals, 
     with ExitStack() as ctx:
         sb = ctx.enter_context(tc.tile_pool(name="sb", bufs=1))
         ps = ctx.enter_context(tc.psum_pool(name="ps", bufs=1))
-        ps2 = ctx.enter_context(tc.psum_pool(name="ps2", bufs=2))
+        ps2 = ctx.enter_context(tc.psum_pool(name="ps2", bufs=3))
 
         list_a = sb.tile([P, SLOTS // 16], U16, name="list_a")
         list_b = sb.tile([P, SLOTS // 16], U16, name="list_b")
         list_v = sb.tile([P, SLOTS // 16], U16, name="list_v")
         kscale = sb.tile([P, T], U8, name="kscale", align_bytes=64)
         kwords = sb.tile([P, T], U32, name="kwords", align_bytes=64)
-        qraw = sb.tile([P, PACK, Q], F32, name="qraw")
+        qraw = sb.tile([P, PACK, Q], F32, name="qraw", align_bytes=64)
         size_col = sb.tile([P, PACK], F32, name="size_col")
         ident = sb.tile([P, P], F32, name="ident")
 
         nc.vector.memset(kscale[:].bitcast(I32), 0)
         make_identity(nc, ident[:])
 
+        nc.sync.dma_start(out=qraw[:], in_=query.rearrange("(p j) q -> p j q", j=PACK))
         nc.sync.dma_start(list_a[:], offs)
         nc.sync.dma_start(list_b[:], offs2)
         for quad in range(4):
-            nc.scalar.dma_start(
+            nc.sync.dma_start(
                 out=kscale[32 * quad : 32 * quad + 4, :].bitcast(I32),
                 in_=keys_scales[0, 4 * quad : 4 * quad + 4, :].bitcast(I32),
             )
-        nc.sync.dma_start(out=qraw[:], in_=query.rearrange("(p j) q -> p j q", j=PACK))
         nc.sync.dma_start(out=kwords[:].bitcast(I32), in_=keys_words[0].rearrange("p n t -> p (n t)").bitcast(I32))
-        vraw = [sb.tile([P, T], F32, name=f"vraw{b}") for b in range(BLOCKS)]
-        nc.sync.dma_start(out=vraw[0][:], in_=vals[0:P, :])
         nc.sync.dma_start(list_v[:], offs3)
         nc.sync.dma_start(out=size_col[:], in_=size.rearrange("o (p t) -> p (o t)", t=PACK))
-        for b in range(1, BLOCKS):
+        vraw = [None] * BLOCKS
+        for b in range(BLOCKS):
+            vraw[b] = sb.tile([P, T], F32, name=f"vraw{b}", tag=f"stage{b}", align_bytes=64)
             nc.sync.dma_start(out=vraw[b][:], in_=vals[b * P : (b + 1) * P, :])
 
         warm = sb.tile([P, 1], F32, name="warm")
         nc.scalar.activation(out=warm[:], in_=ident[:, 0:1], func=ACT.Exp)
         qgrp = sb.tile([P, Q, PACK], BF16, name="qgrp", align_bytes=64)
         nc.scalar.copy(out=qgrp[:], in_=qraw[:].rearrange("p j q -> p q j"))
+        vhalf = sb.tile([P, T], BF16, name="vhalf", align_bytes=64)
+        nc.scalar.activation(out=vhalf[:], in_=vraw[0][:], func=ACT.Copy)
         qcodes = sb.tile([P, Q], U32, name="qcodes", align_bytes=64)
         qscale = sb.tile([P, Q], U8, name="qscale", align_bytes=64)
 
@@ -70,89 +72,87 @@ def tile_attend_synonyms_kernel(tc, query, keys_words, keys_scales, size, vals, 
             g = sb.tile([P, SLOTS], U8, name=f"gs_{name}", align_bytes=64)
             nc.vector.tensor_copy(g[:], kscale[:].indirect(lst[:]))
             gs.append(g)
-        nc.vector.quantize_mx(out=qcodes[:].bitcast(FP8X4), scales=qscale[:], in_=qgrp[:].rearrange("p q j -> p (q j)"))
         scores = []
         for i, (name, lst) in enumerate((("a", list_a), ("b", list_b))):
             g = sb.tile([P, SLOTS], U32, name=f"gw_{name}", align_bytes=64)
-            nc.vector.tensor_copy(g[:], kwords[:].indirect(lst[:]))
             gw.append(g)
             sc = ps.tile([P, SLOTS], F32, name=f"score_{name}")
-            nc.tensor.matmul_mx(out=sc[:], lhsT=qcodes[:].bitcast(FP8X4), lhsT_scale=qscale[:],
-                                rhs=g[:].bitcast(FP8X4), rhs_scale=gs[i][:], start=True, stop=True)
+            width = SLOTS // (i + 1)
+            for c in range(0, SLOTS, width):
+                nc.vector.tensor_copy(g[:, c : c + width], kwords[:].indirect(lst[:, c // 16 : (c + width) // 16]))
+                if i == 0:
+                    nc.vector.quantize_mx(out=qcodes[:].bitcast(FP8X4), scales=qscale[:], in_=qgrp[:].rearrange("p q j -> p (q j)"))
+                nc.tensor.matmul_mx(out=sc[:, c : c + width], lhsT=qcodes[:].bitcast(FP8X4), lhsT_scale=qscale[:],
+                                    rhs=g[:, c : c + width].bitcast(FP8X4), rhs_scale=gs[i][:, c : c + width],
+                                    start=True, stop=True)
             scores.append(sc)
 
         size_bc = ps.tile([P, PACK, P], F32, name="size_bc")
         for t in range(PACK):
             nc.tensor.transpose(size_bc[:, t, :], size_col[:, t : t + 1].to_broadcast([P, P]), ident[:])
 
-        def turn(src, name):
+        def turn(src, dst):
             words = src[:].bitcast(F32)
             turned = ps2.tile([P, 2, P], F32, name="turned")
             for u in range(2):
                 nc.tensor.transpose(turned[:, u, :], words[:, u : 2 * P : 2], ident[:])
-            grp = sb.tile([P, P, PACK], BF16, name=f"grp_{name}", align_bytes=64)
-            nc.scalar.copy(out=grp[:].rearrange("p c t -> p (c t)").bitcast(F32).rearrange("p (c u) -> p c u", u=2),
+            nc.scalar.copy(out=dst.bitcast(F32).rearrange("p (c u) -> p c u", u=2),
                            in_=turned[:].rearrange("p u c -> p c u"))
-            return grp
 
-        def quant(grp, name):
-            codes = sb.tile([P, P], U32, name=f"codes_{name}", align_bytes=64)
-            scales = sb.tile([P, P], U8, name=f"scales_{name}", align_bytes=64)
-            nc.vector.quantize_mx(out=codes[:].bitcast(FP8X4), scales=scales[:], in_=grp[:].rearrange("p c t -> p (c t)"))
-            return codes, scales
+        WIDE = P * PACK
+        grp_early = sb.tile([P, 4 * WIDE], BF16, name="grp_early", align_bytes=64)
+        grp_late = sb.tile([P, WIDE], BF16, name="grp_late", align_bytes=64)
 
-        def gather_v(b):
+        def gather_v(b, dst):
             g = sb.tile([P, SLOTS], BF16, name=f"gv{b}", align_bytes=64)
             nc.vector.tensor_copy(g[:], vraw[b][:].indirect(list_v[:]))
-            return turn(g, f"v{b}")
+            turn(g, dst)
 
-        vg = [None] * BLOCKS
-        vq = [None] * BLOCKS
-        vg[0] = gather_v(0)
-
-        tops = sb.tile([P, 2], F32, name="tops")
+        neg = sb.tile([P, 2 * SLOTS], F32, name="neg")
+        low = None
         for i in range(2):
-            nc.vector.tensor_reduce(out=tops[:, i : i + 1], in_=scores[i][:], axis=AX.X, op=ALU.max)
-        neg_top = sb.tile([P, 1], F32, name="neg_top")
-        nc.vector.tensor_reduce(out=neg_top[:], in_=tops[:], axis=AX.X, op=ALU.max, negate=True)
-        ex = []
-        for i in range(2):
-            e = sb.tile([P, SLOTS], F32, name=f"exp{i}")
-            nc.scalar.activation(out=e[:], in_=scores[i][:], func=ACT.Exp, bias=neg_top[:])
-            ex.append(e)
-        vq[0] = quant(vg[0], "v0")
-        vg[1] = gather_v(1)
-        pair = sb.tile([P, SLOTS], F32, name="pair")
+            nlow = sb.tile([P, 1], F32, name=f"low{i}")
+            nc.vector.tensor_scalar(out=neg[:, i * SLOTS : (i + 1) * SLOTS], in0=scores[i][:], scalar1=-1.0, scalar2=low, op0=ALU.mult, op1=ALU.min,
+                                    accum_out=nlow[:])
+            low = nlow[:]
+        ex = sb.tile([P, 2 * SLOTS], F32, name="ex", tag="stage0", align_bytes=64)
         total = sb.tile([P, 1], F32, name="total")
-        nc.vector.scalar_tensor_tensor(out=pair[:], in0=ex[0][:], scalar=1.0, in1=ex[1][:], op0=ALU.mult, op1=ALU.add,
-                                       accum_out=total[:])
+        nc.scalar.activation(out=ex[:], in_=neg[:], func=ACT.Exp, bias=low, scale=-1.0, accum_out=total[:])
+        gv0 = sb.tile([P, SLOTS], BF16, name="gv0", align_bytes=64)
+        nc.scalar.activation(out=gv0[:], in_=vhalf[:].indirect(list_v[:]), func=ACT.Copy)
+        gather_v(1, grp_early[:, 2 * WIDE : 3 * WIDE])
+        turn(gv0, grp_early[:, WIDE : 2 * WIDE])
         inv = sb.tile([P, 1], F32, name="inv")
         nc.vector.reciprocal(out=inv[:], in_=total[:])
-        vq[1] = quant(vg[1], "v1")
+        pair = sb.tile([P, SLOTS], F32, name="pair")
+        nc.vector.tensor_tensor(out=pair[:], in0=ex[:, 0:SLOTS], in1=ex[:, SLOTS : 2 * SLOTS], op=ALU.add)
         w = sb.tile([P, SLOTS], BF16, name="w", align_bytes=64)
         nc.vector.scalar_tensor_tensor(out=w[:].rearrange("q (p t) -> q p t", t=PACK),
                                        in0=pair[:].rearrange("q (p t) -> q p t", t=PACK), scalar=inv[:],
                                        in1=size_bc[:].rearrange("q t p -> q p t"), op0=ALU.mult, op1=ALU.mult)
-        wg = turn(w, "w")
-        vg[2] = gather_v(2)
-        wcodes, wscales = quant(wg, "w")
-        vq[2] = quant(vg[2], "v2")
+        turn(w, grp_early[:, 0:WIDE])
+        gather_v(2, grp_early[:, 3 * WIDE : 4 * WIDE])
+        gather_v(3, grp_late[:])
 
-        def product(acc, b):
-            nc.tensor.matmul_mx(out=acc, lhsT=wcodes[:].bitcast(FP8X4), lhsT_scale=wscales[:],
-                                rhs=vq[b][0][:].bitcast(FP8X4), rhs_scale=vq[b][1][:], start=True, stop=True)
+        codes = sb.tile([P, 4 * P], U32, name="codes", tag="stage3", align_bytes=64)
+        scales = sb.tile([P, 4 * P], U8, name="scales", align_bytes=64)
+        nc.vector.quantize_mx(out=codes[:].bitcast(FP8X4), scales=scales[:], in_=grp_early[:])
+        codes3 = sb.tile([P, P], U32, name="codes3", align_bytes=64)
+        scales3 = sb.tile([P, P], U8, name="scales3", align_bytes=64)
+        nc.vector.quantize_mx(out=codes3[:].bitcast(FP8X4), scales=scales3[:], in_=grp_late[:])
+
+        def product(acc, c, s):
+            nc.tensor.matmul_mx(out=acc, lhsT=codes[:, 0:P].bitcast(FP8X4), lhsT_scale=scales[:, 0:P],
+                                rhs=c.bitcast(FP8X4), rhs_scale=s, start=True, stop=True)
 
         early = ps.tile([P, 3 * P], F32, name="early")
-        for b in range(3):
-            product(early[:, b * P : (b + 1) * P], b)
+        product(early[:, 0 : 2 * P], codes[:, P : 3 * P], scales[:, P : 3 * P])
+        product(early[:, 2 * P : 3 * P], codes[:, 3 * P : 4 * P], scales[:, 3 * P : 4 * P])
+        late = ps.tile([P, P], F32, name="late")
+        product(late[:], codes3[:], scales3[:])
         early_sb = sb.tile([P, 3 * P], F32, name="early_sb")
         nc.scalar.copy(out=early_sb[:], in_=early[:])
-        nc.sync.dma_start(out=out[:, 0 : 3 * P], in_=early_sb[:])
-
-        vg[3] = gather_v(3)
-        vq[3] = quant(vg[3], "v3")
-        late = ps.tile([P, P], F32, name="late")
-        product(late[:], 3)
+        nc.scalar.dma_start(out=out[:, 0 : 3 * P], in_=early_sb[:])
         late_sb = sb.tile([P, P], F32, name="late_sb")
         nc.vector.tensor_copy(out=late_sb[:], in_=late[:])
         nc.sync.dma_start(out=out[:, 3 * P : 4 * P], in_=late_sb[:])

@@ -76,7 +76,7 @@ def tile_attend_synonyms_kernel(tc, query, keys_words, keys_scales, size, vals, 
         for i, (name, lst) in enumerate((("a", list_a), ("b", list_b))):
             g = sb.tile([P, SLOTS], U32, name=f"gw_{name}", align_bytes=64)
             gw.append(g)
-            sc = ps.tile([P, SLOTS], F32, name=f"score_{name}")
+            sc = ps.tile([P, SLOTS], F32, name=f"score_{name}", tag=f"score_{name}")
             width = SLOTS // (i + 1)
             for c in range(0, SLOTS, width):
                 nc.vector.tensor_copy(g[:, c : c + width], kwords[:].indirect(lst[:, c // 16 : (c + width) // 16]))
@@ -107,6 +107,7 @@ def tile_attend_synonyms_kernel(tc, query, keys_words, keys_scales, size, vals, 
             g = sb.tile([P, SLOTS], BF16, name=f"gv{b}", align_bytes=64)
             nc.vector.tensor_copy(g[:], vraw[b][:].indirect(list_v[:]))
             turn(g, dst)
+            return g
 
         neg = sb.tile([P, 2 * SLOTS], F32, name="neg")
         low = None
@@ -116,27 +117,37 @@ def tile_attend_synonyms_kernel(tc, query, keys_words, keys_scales, size, vals, 
                                     accum_out=nlow[:])
             low = nlow[:]
         ex = sb.tile([P, 2 * SLOTS], F32, name="ex", tag="stage0", align_bytes=64)
-        total = sb.tile([P, 1], F32, name="total")
-        nc.scalar.activation(out=ex[:], in_=neg[:], func=ACT.Exp, bias=low, scale=-1.0, accum_out=total[:])
+        HALF = SLOTS // 2
+        part = sb.tile([P, 2], F32, name="part")
+        for h in range(2):
+            nc.scalar.activation(out=ex[:].rearrange("q (l h s) -> q h l s", l=2, h=2)[:, h],
+                                 in_=neg[:].rearrange("q (l h s) -> q h l s", l=2, h=2)[:, h],
+                                 func=ACT.Exp, bias=low, scale=-1.0, accum_out=part[:, h : h + 1])
         gv0 = sb.tile([P, SLOTS], BF16, name="gv0", align_bytes=64)
         nc.scalar.activation(out=gv0[:], in_=vhalf[:].indirect(list_v[:]), func=ACT.Copy)
         gather_v(1, grp_early[:, 2 * WIDE : 3 * WIDE])
         turn(gv0, grp_early[:, WIDE : 2 * WIDE])
+        pair = sb.tile([P, SLOTS], F32, name="pair")
+        nc.vector.tensor_tensor(out=pair[:, 0:HALF], in0=ex[:, 0:HALF], in1=ex[:, SLOTS : SLOTS + HALF], op=ALU.add)
+        total = sb.tile([P, 1], F32, name="total")
+        nc.vector.tensor_tensor(out=total[:], in0=part[:, 0:1], in1=part[:, 1:2], op=ALU.add)
+        nc.vector.tensor_tensor(out=pair[:, HALF:SLOTS], in0=ex[:, HALF:SLOTS], in1=ex[:, SLOTS + HALF : 2 * SLOTS], op=ALU.add)
         inv = sb.tile([P, 1], F32, name="inv")
         nc.vector.reciprocal(out=inv[:], in_=total[:])
-        pair = sb.tile([P, SLOTS], F32, name="pair")
-        nc.vector.tensor_tensor(out=pair[:], in0=ex[:, 0:SLOTS], in1=ex[:, SLOTS : 2 * SLOTS], op=ALU.add)
         w = sb.tile([P, SLOTS], BF16, name="w", align_bytes=64)
         nc.vector.scalar_tensor_tensor(out=w[:].rearrange("q (p t) -> q p t", t=PACK),
                                        in0=pair[:].rearrange("q (p t) -> q p t", t=PACK), scalar=inv[:],
                                        in1=size_bc[:].rearrange("q t p -> q p t"), op0=ALU.mult, op1=ALU.mult)
         turn(w, grp_early[:, 0:WIDE])
-        gather_v(2, grp_early[:, 3 * WIDE : 4 * WIDE])
-        gather_v(3, grp_late[:])
+        g2 = gather_v(2, grp_early[:, 3 * WIDE : 4 * WIDE])
+        g3 = gather_v(3, grp_late[:])
 
         codes = sb.tile([P, 4 * P], U32, name="codes", tag="stage3", align_bytes=64)
         scales = sb.tile([P, 4 * P], U8, name="scales", align_bytes=64)
-        nc.vector.quantize_mx(out=codes[:].bitcast(FP8X4), scales=scales[:], in_=grp_early[:])
+        for h in range(2):
+            nc.vector.quantize_mx(out=codes[:, 2 * P * h : 2 * P * (h + 1)].bitcast(FP8X4),
+                                  scales=scales[:, 2 * P * h : 2 * P * (h + 1)],
+                                  in_=grp_early[:, 2 * WIDE * h : 2 * WIDE * (h + 1)])
         codes3 = sb.tile([P, P], U32, name="codes3", align_bytes=64)
         scales3 = sb.tile([P, P], U8, name="scales3", align_bytes=64)
         nc.vector.quantize_mx(out=codes3[:].bitcast(FP8X4), scales=scales3[:], in_=grp_late[:])
@@ -145,14 +156,18 @@ def tile_attend_synonyms_kernel(tc, query, keys_words, keys_scales, size, vals, 
             nc.tensor.matmul_mx(out=acc, lhsT=codes[:, 0:P].bitcast(FP8X4), lhsT_scale=scales[:, 0:P],
                                 rhs=c.bitcast(FP8X4), rhs_scale=s, start=True, stop=True)
 
-        early = ps.tile([P, 3 * P], F32, name="early")
-        product(early[:, 0 : 2 * P], codes[:, P : 3 * P], scales[:, P : 3 * P])
-        product(early[:, 2 * P : 3 * P], codes[:, 3 * P : 4 * P], scales[:, 3 * P : 4 * P])
-        late = ps.tile([P, P], F32, name="late")
-        product(late[:], codes3[:], scales3[:])
-        early_sb = sb.tile([P, 3 * P], F32, name="early_sb")
-        nc.scalar.copy(out=early_sb[:], in_=early[:])
-        nc.scalar.dma_start(out=out[:, 0 : 3 * P], in_=early_sb[:])
-        late_sb = sb.tile([P, P], F32, name="late_sb")
-        nc.vector.tensor_copy(out=late_sb[:], in_=late[:])
-        nc.sync.dma_start(out=out[:, 3 * P : 4 * P], in_=late_sb[:])
+        acc0 = ps.tile([P, P], F32, name="acc0", tag="score_a")
+        product(acc0[:], codes[:, P : 2 * P], scales[:, P : 2 * P])
+        acc1 = ps.tile([P, 2 * P], F32, name="acc1", tag="score_b")
+        product(acc1[:], codes[:, 2 * P : 4 * P], scales[:, 2 * P : 4 * P])
+        acc3 = ps.tile([P, P], F32, name="acc3")
+        product(acc3[:], codes3[:], scales3[:])
+        res0 = sb.tile([P, P], F32, name="res0")
+        nc.scalar.copy(out=res0[:], in_=acc0[:])
+        nc.sync.dma_start(out=out[:, 0:P], in_=res0[:])
+        res1 = sb.tile([P, 2 * P], F32, name="res1")
+        nc.vector.tensor_copy(out=res1[:], in_=acc1[:])
+        nc.sync.dma_start(out=out[:, P : 3 * P], in_=res1[:])
+        res3 = sb.tile([P, P], F32, name="res3")
+        nc.scalar.copy(out=res3[:], in_=acc3[:])
+        nc.scalar.dma_start(out=out[:, 3 * P : 4 * P], in_=res3[:])

from contextlib import ExitStack

import concourse.mybir as mybir
from concourse.masks import make_identity

D, T, SLOTS, Q, E = 512, 2048, 512, 128, 512
FLOPS = 2 * (2 * D * Q * SLOTS + SLOTS * Q * E)

F32 = mybir.dt.float32
BF16 = mybir.dt.bfloat16
I32 = mybir.dt.int32
U32 = mybir.dt.uint32
U16 = mybir.dt.uint16
U8 = mybir.dt.uint8
FP8X4 = mybir.dt.float8_e4m3fn_x4
ALU = mybir.AluOpType
ACT = mybir.ActivationFunctionType
AX = mybir.AxisListType

P = 128
PACK = 4
BLOCKS = E // P


def tile_attend_synonyms_kernel(tc, query, keys_words, keys_scales, size, vals, offs, offs2, offs3, out):
    nc = tc.nc
    with ExitStack() as ctx:
        sb = ctx.enter_context(tc.tile_pool(name="sb", bufs=1))
        ps = ctx.enter_context(tc.psum_pool(name="ps", bufs=1))
        ps2 = ctx.enter_context(tc.psum_pool(name="ps2", bufs=3))

        list_a = sb.tile([P, SLOTS // 16], U16, name="list_a")
        list_b = sb.tile([P, SLOTS // 16], U16, name="list_b")
        list_v = sb.tile([P, SLOTS // 16], U16, name="list_v")
        kscale = sb.tile([P, T], U8, name="kscale", align_bytes=64)
        kwords = sb.tile([P, T], U32, name="kwords", align_bytes=64)
        qraw = sb.tile([P, PACK, Q], F32, name="qraw", align_bytes=64)
        size_col = sb.tile([P, PACK], F32, name="size_col")
        ident = sb.tile([P, P], F32, name="ident")

        nc.vector.memset(kscale[:].bitcast(I32), 0)
        make_identity(nc, ident[:])

        nc.sync.dma_start(out=qraw[:], in_=query.rearrange("(p j) q -> p j q", j=PACK))
        nc.sync.dma_start(list_a[:], offs)
        nc.sync.dma_start(list_b[:], offs2)
        for quad in range(4):
            nc.sync.dma_start(
                out=kscale[32 * quad : 32 * quad + 4, :].bitcast(I32),
                in_=keys_scales[0, 4 * quad : 4 * quad + 4, :].bitcast(I32),
            )
        nc.sync.dma_start(out=kwords[:].bitcast(I32), in_=keys_words[0].rearrange("p n t -> p (n t)").bitcast(I32))
        nc.sync.dma_start(list_v[:], offs3)
        nc.sync.dma_start(out=size_col[:], in_=size.rearrange("o (p t) -> p (o t)", t=PACK))
        vraw = [None] * BLOCKS
        for b in range(BLOCKS):
            vraw[b] = sb.tile([P, T], F32, name=f"vraw{b}", tag=f"stage{b}", align_bytes=64)
            nc.sync.dma_start(out=vraw[b][:], in_=vals[b * P : (b + 1) * P, :])

        warm = sb.tile([P, 1], F32, name="warm")
        nc.scalar.activation(out=warm[:], in_=ident[:, 0:1], func=ACT.Exp)
        qgrp = sb.tile([P, Q, PACK], BF16, name="qgrp", align_bytes=64)
        nc.scalar.copy(out=qgrp[:], in_=qraw[:].rearrange("p j q -> p q j"))
        vhalf = sb.tile([P, T], BF16, name="vhalf", align_bytes=64)
        nc.scalar.activation(out=vhalf[:], in_=vraw[0][:], func=ACT.Copy)
        qcodes = sb.tile([P, Q], U32, name="qcodes", align_bytes=64)
        qscale = sb.tile([P, Q], U8, name="qscale", align_bytes=64)

        gs = []
        gw = []
        for name, lst in (("a", list_a), ("b", list_b)):
            g = sb.tile([P, SLOTS], U8, name=f"gs_{name}", align_bytes=64)
            nc.vector.tensor_copy(g[:], kscale[:].indirect(lst[:]))
            gs.append(g)
        scores = []
        for i, (name, lst) in enumerate((("a", list_a), ("b", list_b))):
            g = sb.tile([P, SLOTS], U32, name=f"gw_{name}", align_bytes=64)
            gw.append(g)
            sc = ps.tile([P, SLOTS], F32, name=f"score_{name}", tag=f"score_{name}")
            width = SLOTS // (i + 1)
            for c in range(0, SLOTS, width):
                nc.vector.tensor_copy(g[:, c : c + width], kwords[:].indirect(lst[:, c // 16 : (c + width) // 16]))
                if i == 0:
                    nc.vector.quantize_mx(out=qcodes[:].bitcast(FP8X4), scales=qscale[:], in_=qgrp[:].rearrange("p q j -> p (q j)"))
                nc.tensor.matmul_mx(out=sc[:, c : c + width], lhsT=qcodes[:].bitcast(FP8X4), lhsT_scale=qscale[:],
                                    rhs=g[:, c : c + width].bitcast(FP8X4), rhs_scale=gs[i][:, c : c + width],
                                    start=True, stop=True)
            scores.append(sc)

        size_bc = ps.tile([P, PACK, P], F32, name="size_bc")
        for t in range(PACK):
            nc.tensor.transpose(size_bc[:, t, :], size_col[:, t : t + 1].to_broadcast([P, P]), ident[:])

        def turn(src, dst):
            words = src[:].bitcast(F32)
            turned = ps2.tile([P, 2, P], F32, name="turned")
            for u in range(2):
                nc.tensor.transpose(turned[:, u, :], words[:, u : 2 * P : 2], ident[:])
            nc.scalar.copy(out=dst.bitcast(F32).rearrange("p (c u) -> p c u", u=2),
                           in_=turned[:].rearrange("p u c -> p c u"))

        WIDE = P * PACK
        grp_early = sb.tile([P, 4 * WIDE], BF16, name="grp_early", align_bytes=64)
        grp_late = sb.tile([P, WIDE], BF16, name="grp_late", align_bytes=64)

        def gather_v(b, dst):
            g = sb.tile([P, SLOTS], BF16, name=f"gv{b}", align_bytes=64)
            nc.vector.tensor_copy(g[:], vraw[b][:].indirect(list_v[:]))
            turn(g, dst)
            return g

        neg = sb.tile([P, 2 * SLOTS], F32, name="neg")
        low = None
        for i in range(2):
            nlow = sb.tile([P, 1], F32, name=f"low{i}")
            nc.vector.tensor_scalar(out=neg[:, i * SLOTS : (i + 1) * SLOTS], in0=scores[i][:], scalar1=-1.0, scalar2=low, op0=ALU.mult, op1=ALU.min,
                                    accum_out=nlow[:])
            low = nlow[:]
        ex = sb.tile([P, 2 * SLOTS], F32, name="ex", tag="stage0", align_bytes=64)
        HALF = SLOTS // 2
        part = sb.tile([P, 2], F32, name="part")
        for h in range(2):
            nc.scalar.activation(out=ex[:].rearrange("q (l h s) -> q h l s", l=2, h=2)[:, h],
                                 in_=neg[:].rearrange("q (l h s) -> q h l s", l=2, h=2)[:, h],
                                 func=ACT.Exp, bias=low, scale=-1.0, accum_out=part[:, h : h + 1])
        gv0 = sb.tile([P, SLOTS], BF16, name="gv0", align_bytes=64)
        nc.scalar.activation(out=gv0[:], in_=vhalf[:].indirect(list_v[:]), func=ACT.Copy)
        gather_v(1, grp_early[:, 2 * WIDE : 3 * WIDE])
        turn(gv0, grp_early[:, WIDE : 2 * WIDE])
        pair = sb.tile([P, SLOTS], F32, name="pair")
        nc.vector.tensor_tensor(out=pair[:, 0:HALF], in0=ex[:, 0:HALF], in1=ex[:, SLOTS : SLOTS + HALF], op=ALU.add)
        total = sb.tile([P, 1], F32, name="total")
        nc.vector.tensor_tensor(out=total[:], in0=part[:, 0:1], in1=part[:, 1:2], op=ALU.add)
        nc.vector.tensor_tensor(out=pair[:, HALF:SLOTS], in0=ex[:, HALF:SLOTS], in1=ex[:, SLOTS + HALF : 2 * SLOTS], op=ALU.add)
        inv = sb.tile([P, 1], F32, name="inv")
        nc.vector.reciprocal(out=inv[:], in_=total[:])
        w = sb.tile([P, SLOTS], BF16, name="w", align_bytes=64)
        nc.vector.scalar_tensor_tensor(out=w[:].rearrange("q (p t) -> q p t", t=PACK),
                                       in0=pair[:].rearrange("q (p t) -> q p t", t=PACK), scalar=inv[:],
                                       in1=size_bc[:].rearrange("q t p -> q p t"), op0=ALU.mult, op1=ALU.mult)
        turn(w, grp_early[:, 0:WIDE])
        g2 = gather_v(2, grp_early[:, 3 * WIDE : 4 * WIDE])
        g3 = gather_v(3, grp_late[:])

        codes = sb.tile([P, 4 * P], U32, name="codes", tag="stage3", align_bytes=64)
        scales = sb.tile([P, 4 * P], U8, name="scales", align_bytes=64)
        for h in range(2):
            nc.vector.quantize_mx(out=codes[:, 2 * P * h : 2 * P * (h + 1)].bitcast(FP8X4),
                                  scales=scales[:, 2 * P * h : 2 * P * (h + 1)],
                                  in_=grp_early[:, 2 * WIDE * h : 2 * WIDE * (h + 1)])
        codes3 = sb.tile([P, P], U32, name="codes3", align_bytes=64)
        scales3 = sb.tile([P, P], U8, name="scales3", align_bytes=64)
        nc.vector.quantize_mx(out=codes3[:].bitcast(FP8X4), scales=scales3[:], in_=grp_late[:])

        def product(acc, c, s):
            nc.tensor.matmul_mx(out=acc, lhsT=codes[:, 0:P].bitcast(FP8X4), lhsT_scale=scales[:, 0:P],
                                rhs=c.bitcast(FP8X4), rhs_scale=s, start=True, stop=True)

        acc0 = ps.tile([P, P], F32, name="acc0", tag="score_a")
        product(acc0[:], codes[:, P : 2 * P], scales[:, P : 2 * P])
        acc1 = ps.tile([P, 2 * P], F32, name="acc1", tag="score_b")
        product(acc1[:], codes[:, 2 * P : 4 * P], scales[:, 2 * P : 4 * P])
        acc3 = ps.tile([P, P], F32, name="acc3")
        product(acc3[:], codes3[:], scales3[:])
        res0 = sb.tile([P, P], F32, name="res0")
        nc.scalar.copy(out=res0[:], in_=acc0[:])
        nc.sync.dma_start(out=out[:, 0:P], in_=res0[:])
        res1 = sb.tile([P, 2 * P], F32, name="res1")
        nc.vector.tensor_copy(out=res1[:], in_=acc1[:])
        nc.sync.dma_start(out=out[:, P : 3 * P], in_=res1[:])
        res3 = sb.tile([P, P], F32, name="res3")
        nc.scalar.copy(out=res3[:], in_=acc3[:])
        nc.scalar.dma_start(out=out[:, 3 * P : 4 * P], in_=res3[:])
